import numpy as np
import ml_dtypes


def mxq(x, axis, fmt="e4m3"):
    dtype, down = {"e4m3": (ml_dtypes.float8_e4m3fn, 7), "e5m2": (ml_dtypes.float8_e5m2, 14)}[fmt]
    v = np.moveaxis(np.asarray(x, np.float32).astype(ml_dtypes.bfloat16).astype(np.float64), axis, -1)
    blocks = v.reshape(v.shape[:-1] + (-1, 32))
    amax = np.abs(blocks).max(-1, keepdims=True)
    byte = np.maximum(np.where(amax > 0, np.frexp(amax)[1] - 1 + 127, 0) - down, 1)
    scale = np.exp2(byte - 127.0)
    codes = (blocks / scale).astype(np.float32).astype(dtype).astype(np.float64)
    return np.moveaxis((codes * scale).reshape(v.shape), -1, axis)


WIDE = False


def mx_kscale(k):
    if not WIDE:
        return np.ones(k)
    levels = np.array([10, -10, 5, -5, 0])
    if k % 512:
        return np.exp2(np.random.permutation(np.resize(levels, k // 32))).repeat(32)
    a = np.empty((k // 512, 16))
    for p in range(k // 512):
        a[p, :8] = np.random.permutation(np.resize(levels, 8))
        for g in range(8):
            far = levels[np.abs(levels - a[p, g]) >= 10]
            a[p, g + 8] = far[np.random.randint(len(far))]
    return np.exp2(a.ravel()).repeat(32)


def f64(x):
    return np.asarray(x).astype(np.float64)


def striped(idx):
    return np.tile(idx.reshape(-1, 16).T, (8, 1)).astype(np.uint16)


def unstriped(offs):
    return offs[:16].T.reshape(-1).astype(np.int64)


def gelu(v):
    return 0.5 * v * (1.0 + np.tanh(np.sqrt(2.0 / np.pi) * (v + 0.044715 * v**3)))


K, T, E, C, H, N = 2048, 1024, 2, 256, 512, 256


def by_expert(wq, xq):
    return np.concatenate([wq[e].T @ xq[:, e * C:(e + 1) * C] for e in range(E)], axis=1)


def setup_inputs():
    n = np.random.standard_normal
    s = mx_kscale(K)[:, None]
    u = mx_kscale(H)
    return {
        "xT": (n((K, T)) * s).astype(np.float32),
        "w1": (n((E, K, H)) / np.sqrt(K) / s[None] * u[None, None, :]).astype(np.float32),
        "w2": (n((E, H, N)) / np.sqrt(H) / u[None, :, None]).astype(np.float32),
        "gate": np.tile(np.random.uniform(0.2, 1.0, E * C), (N, 1)).astype(np.float32),
        "offs": striped(np.random.permutation(T)[:E * C]),
    }


def reference(xT, w1, w2, gate, offs):
    idx = unstriped(offs)
    xq = mxq(f64(xT)[:, idx], 0, "e4m3")
    h = gelu(by_expert(mxq(f64(w1), 1, "e4m3"), xq))
    y = by_expert(mxq(f64(w2), 1, "e4m3"), mxq(h, 0, "e4m3"))
    out = np.zeros((N, T))
    out[:, idx] = f64(gate) * y
    return out

@@ -1,0 +1,207 @@
+from contextlib import ExitStack
+
+import concourse.mybir as mybir
+
+K, T, E, C, H, N = 2048, 1024, 2, 256, 512, 256
+SLOTS = E * C
+FLOPS = 2 * SLOTS * (K * H + H * N)
+
+F32 = mybir.dt.float32
+BF16 = mybir.dt.bfloat16
+U32 = mybir.dt.uint32
+U16 = mybir.dt.uint16
+U8 = mybir.dt.uint8
+I32 = mybir.dt.int32
+FP8X4 = mybir.dt.float8_e4m3fn_x4
+GELU = mybir.ActivationFunctionType.Gelu_apprx_tanh
+MULT = mybir.AluOpType.mult
+ADD = mybir.AluOpType.add
+
+P = 128
+PACK = 4
+K_PASS = P * PACK
+PASSES = K // K_PASS
+NB = N // P
+
+X_SCALAR_TOKENS = 768
+RAW_BUFS = 10
+
+
+def tile_routed_moe_kernel(tc, xT, w1, w2, gate, offs, out):
+    nc = tc.nc
+    with ExitStack() as ctx:
+        lists = ctx.enter_context(tc.tile_pool(name="lists", bufs=1))
+        keep = ctx.enter_context(tc.tile_pool(name="keep", bufs=1))
+        raw_pool = ctx.enter_context(tc.tile_pool(name="raw", bufs=RAW_BUFS))
+        stage = ctx.enter_context(tc.tile_pool(name="stage", bufs=3))
+        psum_a = ctx.enter_context(tc.psum_pool(name="psum_a", bufs=6))
+        psum_y = ctx.enter_context(tc.psum_pool(name="psum_y", bufs=2))
+
+        offs_t = lists.tile([P, SLOTS // 16], U16, name="offs_t")
+
+        x_view = xT.rearrange("(g p u e) n -> g u p (e n)", p=P, u=2, e=2)
+        w1_view = w1.rearrange("x (g p j) c -> x g p (j c)", p=P, j=PACK)
+        x_raw = {}
+        w1_raw = {}
+        w2_raw = {}
+        gate_t = {}
+
+        def load_x(g, u):
+            t = raw_pool.tile([P, 2 * T], F32, name="xraw%d%d" % (g, u), tag="raw")
+            nc.sync.dma_start(out=t[:], in_=x_view[g, u])
+            x_raw[(g, u)] = t
+
+        def load_w1(e, g):
+            t = raw_pool.tile([P, PACK * H], F32, name="w1raw%d%d" % (e, g), tag="raw")
+            nc.sync.dma_start(out=t[:], in_=w1_view[e, g])
+            w1_raw[(e, g)] = t
+
+        def load_w2_gate(e):
+            t = keep.tile([P, PACK, N], F32, name="w2raw%d" % e)
+            nc.sync.dma_start(out=t[:], in_=w2[e].rearrange("(p j) n -> p j n", j=PACK))
+            w2_raw[e] = t
+            gt = keep.tile([P, NB, C], F32, name="gate%d" % e)
+            nc.sync.dma_start(out=gt[:], in_=gate[:, e * C:(e + 1) * C].rearrange("(b p) s -> p b s", p=P))
+            gate_t[e] = gt
+
+        load_x(0, 0)
+        nc.sync.dma_start(offs_t[:], offs)
+        for g in range(PASSES):
+            for u in range(2):
+                if (g, u) != (0, 0):
+                    load_x(g, u)
+        for g in range(PASSES):
+            load_w1(0, g)
+        load_w2_gate(0)
+        for g in range(PASSES):
+            load_w1(1, g)
+        load_w2_gate(1)
+
+        warm_in = keep.tile([P, 8], F32, name="warm_in")
+        warm_out = keep.tile([P, 8], F32, name="warm_out")
+        nc.gpsimd.memset(warm_in[:], 0.0)
+        nc.scalar.activation(out=warm_out[:], in_=warm_in[:], func=GELU)
+        win = []
+        for b in range(NB):
+            wt = keep.tile([P, T], F32, name="win%d" % b)
+            nc.gpsimd.memset(wt[:], 0.0)
+            win.append(wt)
+
+        x_codes = []
+        x_scales = []
+        x_words = {}
+        x_grouped = {}
+
+        def x_cast_gather(g, u):
+            if u == 0:
+                x_words[g] = stage.tile([P, 2, SLOTS, 2], BF16, name="xw", tag="xw", bufs=2)
+            pairs = stage.tile([P, T, 2], BF16, name="pairs", tag="pairs", bufs=4)
+            src = x_raw[(g, u)][:].rearrange("p (e n) -> p n e", e=2)
+            cs = X_SCALAR_TOKENS
+            nc.scalar.copy(out=pairs[:, 0:cs, :], in_=src[:, 0:cs, :])
+            nc.gpsimd.tensor_scalar(out=pairs[:, cs:T, :], in0=src[:, cs:T, :], scalar1=1.0, scalar2=0.0, op0=MULT, op1=ADD)
+            window = pairs[:].rearrange("p n e -> p (n e)").bitcast(U32)
+            dst = x_words[g][:].rearrange("p u s e -> p (u s e)").bitcast(U32).rearrange("p (u s) -> p u s", u=2)
+            nc.vector.tensor_copy(out=dst[:, u, :], in_=window.indirect(offs_t[:]))
+
+        def x_interleave(g):
+            xg = stage.tile([P, SLOTS, PACK], BF16, name="xg", tag="xg", bufs=2, align_bytes=64)
+            nc.vector.tensor_copy(
+                out=xg[:].rearrange("p s t -> p (s t)").bitcast(I32).rearrange("p (s u) -> p s u", u=2),
+                in_=x_words[g][:].rearrange("p u s e -> p (u s e)").bitcast(I32).rearrange("p (u s) -> p s u", u=2),
+            )
+            x_grouped[g] = xg
+
+        def x_quantize(g):
+            xc = keep.tile([P, SLOTS], U32, name="xc%d" % g, align_bytes=64)
+            xs = keep.tile([P, SLOTS], U8, name="xs%d" % g, align_bytes=64)
+            nc.vector.quantize_mx(out=xc[:].bitcast(FP8X4), scales=xs[:], in_=x_grouped[g][:].rearrange("p s t -> p (s t)"))
+            x_codes.append(xc)
+            x_scales.append(xs)
+
+        for g in range(PASSES):
+            x_cast_gather(g, 0)
+            if g > 0:
+                x_interleave(g - 1)
+            x_cast_gather(g, 1)
+            if g > 0:
+                x_quantize(g - 1)
+        x_interleave(PASSES - 1)
+        x_quantize(PASSES - 1)
+
+        y_tiles = {}
+        for e in range(E):
+            slots = slice(e * C, (e + 1) * C)
+            acc = [psum_a.tile([P, C], F32, name="a%d%d" % (e, t), tag="a") for t in range(PACK)]
+            for g in range(PASSES):
+                wg = stage.tile([P, PACK * H], BF16, name="wg", tag="wg", bufs=3, align_bytes=64)
+                dst = wg[:].rearrange("p (t m j) -> p m j t", t=PACK, j=PACK)
+                src = w1_raw[(e, g)][:].rearrange("p (j m t) -> p m j t", j=PACK, t=PACK)
+                last = g == PASSES - 1
+                ms = 44 if last else (96 if e == 0 else 112)
+                if last:
+                    nc.vector.tensor_copy(out=dst[:, :, :, 0:2], in_=src[:, :, :, 0:2])
+                    nc.scalar.copy(out=dst[:, :, :, 2:4], in_=src[:, :, :, 2:4])
+                else:
+                    nc.scalar.copy(out=dst[:, P - ms:P], in_=src[:, P - ms:P])
+                    nc.vector.tensor_copy(out=dst[:, 0:P - ms], in_=src[:, 0:P - ms])
+                wc = keep.tile([P, H], U32, name="w1c%d%d" % (e, g), align_bytes=64)
+                ws = keep.tile([P, H], U8, name="w1s%d%d" % (e, g), align_bytes=64)
+                if last:
+                    for hf in range(2):
+                        nc.vector.quantize_mx(
+                            out=wc[:, hf * 256:(hf + 1) * 256].bitcast(FP8X4), scales=ws[:, hf * 256:(hf + 1) * 256],
+                            in_=wg[:, hf * 1024:(hf + 1) * 1024])
+                else:
+                    nc.vector.quantize_mx(out=wc[:].bitcast(FP8X4), scales=ws[:], in_=wg[:])
+                for t in range(PACK):
+                    cols = slice(t * P, (t + 1) * P)
+                    nc.tensor.matmul_mx(
+                        out=acc[t][:],
+                        lhsT=wc[:, cols].bitcast(FP8X4), lhsT_scale=ws[:, cols],
+                        rhs=x_codes[g][:, slots].bitcast(FP8X4), rhs_scale=x_scales[g][:, slots],
+                        start=(g == 0), stop=(g == PASSES - 1),
+                    )
+
+            w2g = keep.tile([P, N, PACK], BF16, name="w2g%d" % e, align_bytes=64)
+            if e == 0:
+                nc.scalar.copy(out=w2g[:], in_=w2_raw[e][:].rearrange("p j n -> p n j"))
+            else:
+                nc.vector.tensor_copy(out=w2g[:], in_=w2_raw[e][:].rearrange("p j n -> p n j"))
+            w2c = keep.tile([P, N], U32, name="w2c%d" % e, align_bytes=64)
+            w2s = keep.tile([P, N], U8, name="w2s%d" % e, align_bytes=64)
+            nc.vector.quantize_mx(out=w2c[:].bitcast(FP8X4), scales=w2s[:], in_=w2g[:].rearrange("p n j -> p (n j)"))
+
+            h_planes = keep.tile([P, PACK, C], BF16, name="hp%d" % e)
+            for t in range(PACK):
+                nc.scalar.activation(out=h_planes[:, t, :], in_=acc[t][:], func=GELU)
+            hg = keep.tile([P, C, PACK], BF16, name="hg%d" % e, align_bytes=64)
+            nc.vector.tensor_copy(out=hg[:], in_=h_planes[:].rearrange("p t s -> p s t"))
+            hc = keep.tile([P, C], U32, name="hc%d" % e, align_bytes=64)
+            hs = keep.tile([P, C], U8, name="hs%d" % e, align_bytes=64)
+            nc.vector.quantize_mx(out=hc[:].bitcast(FP8X4), scales=hs[:], in_=hg[:].rearrange("p s t -> p (s t)"))
+
+            for b in range(NB):
+                cols = slice(b * P, (b + 1) * P)
+                y = psum_y.tile([P, C], F32, name="y%d%d" % (e, b), tag="y")
+                nc.tensor.matmul_mx(
+                    out=y[:],
+                    lhsT=w2c[:, cols].bitcast(FP8X4), lhsT_scale=w2s[:, cols],
+                    rhs=hc[:].bitcast(FP8X4), rhs_scale=hs[:],
+                    start=True, stop=True,
+                )
+                y_sb = keep.tile([P, C], F32, name="ysb%d%d" % (e, b))
+                if e == E - 1 and b == 0:
+                    nc.vector.tensor_copy(out=y_sb[:], in_=y[:])
+                else:
+                    nc.scalar.copy(out=y_sb[:], in_=y[:])
+                y_tiles[(e, b)] = y_sb
+
+        for e in range(E):
+            for b in range(NB):
+                nc.vector.tensor_tensor(
+                    out=win[b][:].indirect(offs_t[:, e * (C // 16):(e + 1) * (C // 16)]),
+                    in0=y_tiles[(e, b)][:], in1=gate_t[e][:, b, :], op=MULT,
+                )
+                if e == E - 1:
+                    nc.sync.dma_start(out=out[b * P:(b + 1) * P, :], in_=win[b][:])

@@ -165,9 +165,9 @@ def tile_routed_moe_kernel(tc, xT, w1, w2, gate, offs, out):
 
             w2g = keep.tile([P, N, PACK], BF16, name="w2g%d" % e, align_bytes=64)
             if e == 0:
-                nc.scalar.copy(out=w2g[:], in_=w2_raw[e][:].rearrange("p j n -> p n j"))
+                nc.scalar.copy(out=w2g[:].rearrange("p (c i) j -> p c j i", i=4), in_=w2_raw[e][:].rearrange("p j (c i) -> p c j i", i=4))
             else:
-                nc.vector.tensor_copy(out=w2g[:], in_=w2_raw[e][:].rearrange("p j n -> p n j"))
+                nc.vector.tensor_copy(out=w2g[:].rearrange("p (c i) j -> p c j i", i=4), in_=w2_raw[e][:].rearrange("p j (c i) -> p c j i", i=4))
             w2c = keep.tile([P, N], U32, name="w2c%d" % e, align_bytes=64)
             w2s = keep.tile([P, N], U8, name="w2s%d" % e, align_bytes=64)
             nc.vector.quantize_mx(out=w2c[:].bitcast(FP8X4), scales=w2s[:], in_=w2g[:].rearrange("p n j -> p (n j)"))
@@ -176,7 +176,7 @@ def tile_routed_moe_kernel(tc, xT, w1, w2, gate, offs, out):
             for t in range(PACK):
                 nc.scalar.activation(out=h_planes[:, t, :], in_=acc[t][:], func=GELU)
             hg = keep.tile([P, C, PACK], BF16, name="hg%d" % e, align_bytes=64)
-            nc.vector.tensor_copy(out=hg[:], in_=h_planes[:].rearrange("p t s -> p s t"))
+            nc.vector.tensor_copy(out=hg[:].rearrange("p (c i) t -> p c t i", i=4), in_=h_planes[:].rearrange("p t (c i) -> p c t i", i=4))
             hc = keep.tile([P, C], U32, name="hc%d" % e, align_bytes=64)
             hs = keep.tile([P, C], U8, name="hs%d" % e, align_bytes=64)
             nc.vector.quantize_mx(out=hc[:].bitcast(FP8X4), scales=hs[:], in_=hg[:].rearrange("p s t -> p (s t)"))
@@ -191,10 +191,7 @@ def tile_routed_moe_kernel(tc, xT, w1, w2, gate, offs, out):
                     start=True, stop=True,
                 )
                 y_sb = keep.tile([P, C], F32, name="ysb%d%d" % (e, b))
-                if e == E - 1 and b == 0:
-                    nc.vector.tensor_copy(out=y_sb[:], in_=y[:])
-                else:
-                    nc.scalar.copy(out=y_sb[:], in_=y[:])
+                nc.scalar.copy(out=y_sb[:], in_=y[:])
                 y_tiles[(e, b)] = y_sb
 
         for e in range(E):

@@ -135,13 +135,13 @@ def tile_routed_moe_kernel(tc, xT, w1, w2, gate, offs, out):
             acc = [psum_a.tile([P, C], F32, name="a%d%d" % (e, t), tag="a") for t in range(PACK)]
             for g in range(PASSES):
                 wg = stage.tile([P, PACK * H], BF16, name="wg", tag="wg", bufs=3, align_bytes=64)
-                dst = wg[:].rearrange("p (t m j) -> p m j t", t=PACK, j=PACK)
-                src = w1_raw[(e, g)][:].rearrange("p (j m t) -> p m j t", j=PACK, t=PACK)
+                dst = wg[:].rearrange("p (t m a b) -> p m a t b", t=PACK, a=2, b=2)
+                src = w1_raw[(e, g)][:].rearrange("p (a b m t) -> p m a t b", a=2, b=2, t=PACK)
                 last = g == PASSES - 1
                 ms = 44 if last else (96 if e == 0 else 112)
                 if last:
-                    nc.vector.tensor_copy(out=dst[:, :, :, 0:2], in_=src[:, :, :, 0:2])
-                    nc.scalar.copy(out=dst[:, :, :, 2:4], in_=src[:, :, :, 2:4])
+                    nc.vector.tensor_copy(out=dst[:, :, :, 0:2, :], in_=src[:, :, :, 0:2, :])
+                    nc.scalar.copy(out=dst[:, :, :, 2:4, :], in_=src[:, :, :, 2:4, :])
                 else:
                     nc.scalar.copy(out=dst[:, P - ms:P], in_=src[:, P - ms:P])
                     nc.vector.tensor_copy(out=dst[:, 0:P - ms], in_=src[:, 0:P - ms])

@@ -25,6 +25,7 @@ NB = N // P
 
 X_SCALAR_TOKENS = 768
 RAW_BUFS = 10
+H_VECTOR_SLOTS = 160
 
 
 def tile_routed_moe_kernel(tc, xT, w1, w2, gate, offs, out):
@@ -176,7 +177,14 @@ def tile_routed_moe_kernel(tc, xT, w1, w2, gate, offs, out):
             for t in range(PACK):
                 nc.scalar.activation(out=h_planes[:, t, :], in_=acc[t][:], func=GELU)
             hg = keep.tile([P, C, PACK], BF16, name="hg%d" % e, align_bytes=64)
-            nc.vector.tensor_copy(out=hg[:].rearrange("p (c i) t -> p c t i", i=4), in_=h_planes[:].rearrange("p t (c i) -> p c t i", i=4))
+            il_dst = hg[:].rearrange("p (c i) t -> p c t i", i=4)
+            il_src = h_planes[:].rearrange("p t (c i) -> p c t i", i=4)
+            if e == E - 1:
+                cv = H_VECTOR_SLOTS // 4
+                nc.vector.tensor_copy(out=il_dst[:, 0:cv], in_=il_src[:, 0:cv])
+                nc.scalar.copy(out=il_dst[:, cv:C // 4], in_=il_src[:, cv:C // 4])
+            else:
+                nc.vector.tensor_copy(out=il_dst, in_=il_src)
             hc = keep.tile([P, C], U32, name="hc%d" % e, align_bytes=64)
             hs = keep.tile([P, C], U8, name="hs%d" % e, align_bytes=64)
             nc.vector.quantize_mx(out=hc[:].bitcast(FP8X4), scales=hs[:], in_=hg[:].rearrange("p s t -> p (s t)"))

@@ -165,10 +165,7 @@ def tile_routed_moe_kernel(tc, xT, w1, w2, gate, offs, out):
                     )
 
             w2g = keep.tile([P, N, PACK], BF16, name="w2g%d" % e, align_bytes=64)
-            if e == 0:
-                nc.scalar.copy(out=w2g[:].rearrange("p (c i) j -> p c j i", i=4), in_=w2_raw[e][:].rearrange("p j (c i) -> p c j i", i=4))
-            else:
-                nc.vector.tensor_copy(out=w2g[:].rearrange("p (c i) j -> p c j i", i=4), in_=w2_raw[e][:].rearrange("p j (c i) -> p c j i", i=4))
+            nc.vector.tensor_copy(out=w2g[:].rearrange("p (c i) j -> p c j i", i=4), in_=w2_raw[e][:].rearrange("p j (c i) -> p c j i", i=4))
             w2c = keep.tile([P, N], U32, name="w2c%d" % e, align_bytes=64)
             w2s = keep.tile([P, N], U8, name="w2s%d" % e, align_bytes=64)
             nc.vector.quantize_mx(out=w2c[:].bitcast(FP8X4), scales=w2s[:], in_=w2g[:].rearrange("p n j -> p (n j)"))

@@ -53,6 +53,12 @@ def tile_routed_moe_kernel(tc, xT, w1, w2, gate, offs, out):
             x_raw[(g, u)] = t
 
         def load_w1(e, g):
+            if (e, g) == (E - 1, PASSES - 1):
+                for v in range(2):
+                    t = raw_pool.tile([P, 2 * H], F32, name="w1raw%d%d%d" % (e, g, v), tag="raw")
+                    nc.sync.dma_start(out=t[:], in_=w1_view[e, g][:, v * 2 * H:(v + 1) * 2 * H])
+                    w1_raw[(e, g, v)] = t
+                return
             t = raw_pool.tile([P, PACK * H], F32, name="w1raw%d%d" % (e, g), tag="raw")
             nc.sync.dma_start(out=t[:], in_=w1_view[e, g])
             w1_raw[(e, g)] = t
@@ -137,10 +143,19 @@ def tile_routed_moe_kernel(tc, xT, w1, w2, gate, offs, out):
             for g in range(PASSES):
                 wg = stage.tile([P, PACK * H], BF16, name="wg", tag="wg", bufs=3, align_bytes=64)
                 dst = wg[:].rearrange("p (t m a b) -> p m a t b", t=PACK, a=2, b=2)
-                src = w1_raw[(e, g)][:].rearrange("p (a b m t) -> p m a t b", a=2, b=2, t=PACK)
                 last = g == PASSES - 1
                 ms = 44 if last else (96 if e == 0 else 112)
-                if last:
+                if (e, g) == (E - 1, PASSES - 1):
+                    for v in range(2):
+                        half = w1_raw[(e, g, v)][:].rearrange("p (b m t) -> p m t b", b=2, t=PACK)
+                        nc.vector.tensor_copy(out=dst[:, :, v, 0:2, :], in_=half[:, :, 0:2, :])
+                        nc.scalar.copy(out=dst[:, :, v, 2:4, :], in_=half[:, :, 2:4, :])
+                    src = None
+                else:
+                    src = w1_raw[(e, g)][:].rearrange("p (a b m t) -> p m a t b", a=2, b=2, t=PACK)
+                if src is None:
+                    src = None
+                elif last:
                     nc.vector.tensor_copy(out=dst[:, :, :, 0:2, :], in_=src[:, :, :, 0:2, :])
                     nc.scalar.copy(out=dst[:, :, :, 2:4, :], in_=src[:, :, :, 2:4, :])
                 else:

@@ -25,7 +25,7 @@ NB = N // P
 
 X_SCALAR_TOKENS = 768
 RAW_BUFS = 10
-H_VECTOR_SLOTS = 160
+HALF = C // 2
 
 
 def tile_routed_moe_kernel(tc, xT, w1, w2, gate, offs, out):
@@ -35,8 +35,8 @@ def tile_routed_moe_kernel(tc, xT, w1, w2, gate, offs, out):
         keep = ctx.enter_context(tc.tile_pool(name="keep", bufs=1))
         raw_pool = ctx.enter_context(tc.tile_pool(name="raw", bufs=RAW_BUFS))
         stage = ctx.enter_context(tc.tile_pool(name="stage", bufs=3))
-        psum_a = ctx.enter_context(tc.psum_pool(name="psum_a", bufs=6))
-        psum_y = ctx.enter_context(tc.psum_pool(name="psum_y", bufs=2))
+        psum_a = ctx.enter_context(tc.psum_pool(name="psum_a", bufs=4))
+        psum_y = ctx.enter_context(tc.psum_pool(name="psum_y", bufs=4))
 
         offs_t = lists.tile([P, SLOTS // 16], U16, name="offs_t")
 
@@ -138,8 +138,7 @@ def tile_routed_moe_kernel(tc, xT, w1, w2, gate, offs, out):
 
         y_tiles = {}
         for e in range(E):
-            slots = slice(e * C, (e + 1) * C)
-            acc = [psum_a.tile([P, C], F32, name="a%d%d" % (e, t), tag="a") for t in range(PACK)]
+            acc = [psum_a.tile([P, PACK, HALF], F32, name="a%d%d" % (e, half), tag="a") for half in range(2)]
             for g in range(PASSES):
                 wg = stage.tile([P, PACK * H], BF16, name="wg", tag="wg", bufs=3, align_bytes=64)
                 dst = wg[:].rearrange("p (t m a b) -> p m a t b", t=PACK, a=2, b=2)
@@ -154,7 +153,7 @@ def tile_routed_moe_kernel(tc, xT, w1, w2, gate, offs, out):
                 else:
                     src = w1_raw[(e, g)][:].rearrange("p (a b m t) -> p m a t b", a=2, b=2, t=PACK)
                 if src is None:
-                    src = None
+                    pass
                 elif last:
                     nc.vector.tensor_copy(out=dst[:, :, :, 0:2, :], in_=src[:, :, :, 0:2, :])
                     nc.scalar.copy(out=dst[:, :, :, 2:4, :], in_=src[:, :, :, 2:4, :])
@@ -170,14 +169,17 @@ def tile_routed_moe_kernel(tc, xT, w1, w2, gate, offs, out):
                             in_=wg[:, hf * 1024:(hf + 1) * 1024])
                 else:
                     nc.vector.quantize_mx(out=wc[:].bitcast(FP8X4), scales=ws[:], in_=wg[:])
-                for t in range(PACK):
-                    cols = slice(t * P, (t + 1) * P)
-                    nc.tensor.matmul_mx(
-                        out=acc[t][:],
-                        lhsT=wc[:, cols].bitcast(FP8X4), lhsT_scale=ws[:, cols],
-                        rhs=x_codes[g][:, slots].bitcast(FP8X4), rhs_scale=x_scales[g][:, slots],
-                        start=(g == 0), stop=(g == PASSES - 1),
-                    )
+                for pair in range(2):
+                    for half in range(2):
+                        hs0 = e * C + half * HALF
+                        for t in (2 * pair, 2 * pair + 1):
+                            cols = slice(t * P, (t + 1) * P)
+                            nc.tensor.matmul_mx(
+                                out=acc[half][:, t, :],
+                                lhsT=wc[:, cols].bitcast(FP8X4), lhsT_scale=ws[:, cols],
+                                rhs=x_codes[g][:, hs0:hs0 + HALF].bitcast(FP8X4), rhs_scale=x_scales[g][:, hs0:hs0 + HALF],
+                                start=(g == 0 and t == 0), stop=(g == PASSES - 1 and t == PACK - 1),
+                            )
 
             w2g = keep.tile([P, N, PACK], BF16, name="w2g%d" % e, align_bytes=64)
             nc.vector.tensor_copy(out=w2g[:].rearrange("p (c i) j -> p c j i", i=4), in_=w2_raw[e][:].rearrange("p j (c i) -> p c j i", i=4))
@@ -185,33 +187,27 @@ def tile_routed_moe_kernel(tc, xT, w1, w2, gate, offs, out):
             w2s = keep.tile([P, N], U8, name="w2s%d" % e, align_bytes=64)
             nc.vector.quantize_mx(out=w2c[:].bitcast(FP8X4), scales=w2s[:], in_=w2g[:].rearrange("p n j -> p (n j)"))
 
-            h_planes = keep.tile([P, PACK, C], BF16, name="hp%d" % e)
-            for t in range(PACK):
-                nc.scalar.activation(out=h_planes[:, t, :], in_=acc[t][:], func=GELU)
             hg = keep.tile([P, C, PACK], BF16, name="hg%d" % e, align_bytes=64)
-            il_dst = hg[:].rearrange("p (c i) t -> p c t i", i=4)
-            il_src = h_planes[:].rearrange("p t (c i) -> p c t i", i=4)
-            if e == E - 1:
-                cv = H_VECTOR_SLOTS // 4
-                nc.vector.tensor_copy(out=il_dst[:, 0:cv], in_=il_src[:, 0:cv])
-                nc.scalar.copy(out=il_dst[:, cv:C // 4], in_=il_src[:, cv:C // 4])
-            else:
-                nc.vector.tensor_copy(out=il_dst, in_=il_src)
             hc = keep.tile([P, C], U32, name="hc%d" % e, align_bytes=64)
             hs = keep.tile([P, C], U8, name="hs%d" % e, align_bytes=64)
-            nc.vector.quantize_mx(out=hc[:].bitcast(FP8X4), scales=hs[:], in_=hg[:].rearrange("p s t -> p (s t)"))
-
+            y = [psum_y.tile([P, C], F32, name="y%d%d" % (e, b), tag="y") for b in range(NB)]
+            for half in range(2):
+                hslots = slice(half * HALF, (half + 1) * HALF)
+                nc.scalar.activation(out=hg[:, hslots, :], in_=acc[half][:].rearrange("p t s -> p s t"), func=GELU)
+                nc.vector.quantize_mx(
+                    out=hc[:, hslots].bitcast(FP8X4), scales=hs[:, hslots],
+                    in_=hg[:, hslots, :].rearrange("p s t -> p (s t)"))
+                for b in range(NB):
+                    cols = slice(b * P, (b + 1) * P)
+                    nc.tensor.matmul_mx(
+                        out=y[b][:, hslots],
+                        lhsT=w2c[:, cols].bitcast(FP8X4), lhsT_scale=w2s[:, cols],
+                        rhs=hc[:, hslots].bitcast(FP8X4), rhs_scale=hs[:, hslots],
+                        start=True, stop=True,
+                    )
             for b in range(NB):
-                cols = slice(b * P, (b + 1) * P)
-                y = psum_y.tile([P, C], F32, name="y%d%d" % (e, b), tag="y")
-                nc.tensor.matmul_mx(
-                    out=y[:],
-                    lhsT=w2c[:, cols].bitcast(FP8X4), lhsT_scale=w2s[:, cols],
-                    rhs=hc[:].bitcast(FP8X4), rhs_scale=hs[:],
-                    start=True, stop=True,
-                )
                 y_sb = keep.tile([P, C], F32, name="ysb%d%d" % (e, b))
-                nc.scalar.copy(out=y_sb[:], in_=y[:])
+                nc.scalar.copy(out=y_sb[:], in_=y[b][:])
                 y_tiles[(e, b)] = y_sb
 
         for e in range(E):

@@ -25,6 +25,8 @@ NB = N // P
 
 X_SCALAR_TOKENS = 768
 RAW_BUFS = 10
+SCALAR_M = [[96, 96, 96, 0], [0, 128, 128, 0]]
+LAST_VECTOR_M = 40
 HALF = C // 2
 
 
@@ -55,8 +57,8 @@ def tile_routed_moe_kernel(tc, xT, w1, w2, gate, offs, out):
         def load_w1(e, g):
             if (e, g) == (E - 1, PASSES - 1):
                 for v in range(2):
-                    t = raw_pool.tile([P, 2 * H], F32, name="w1raw%d%d%d" % (e, g, v), tag="raw")
-                    nc.sync.dma_start(out=t[:], in_=w1_view[e, g][:, v * 2 * H:(v + 1) * 2 * H])
+                    t = raw_pool.tile([P, PACK, H // 2], F32, name="w1raw%d%d%d" % (e, g, v), tag="raw")
+                    nc.sync.dma_start(out=t[:], in_=w1[e, g * K_PASS:(g + 1) * K_PASS, v * (H // 2):(v + 1) * (H // 2)].rearrange("(p j) c -> p j c", j=PACK))
                     w1_raw[(e, g, v)] = t
                 return
             t = raw_pool.tile([P, PACK * H], F32, name="w1raw%d%d" % (e, g), tag="raw")
@@ -136,19 +138,21 @@ def tile_routed_moe_kernel(tc, xT, w1, w2, gate, offs, out):
         x_interleave(PASSES - 1)
         x_quantize(PASSES - 1)
 
-        y_tiles = {}
+        y_parts = {(e, b): [] for e in range(E) for b in range(NB)}
         for e in range(E):
             acc = [psum_a.tile([P, PACK, HALF], F32, name="a%d%d" % (e, half), tag="a") for half in range(2)]
             for g in range(PASSES):
                 wg = stage.tile([P, PACK * H], BF16, name="wg", tag="wg", bufs=3, align_bytes=64)
                 dst = wg[:].rearrange("p (t m a b) -> p m a t b", t=PACK, a=2, b=2)
                 last = g == PASSES - 1
-                ms = 44 if last else (96 if e == 0 else 112)
+                ms = SCALAR_M[e][g]
                 if (e, g) == (E - 1, PASSES - 1):
                     for v in range(2):
-                        half = w1_raw[(e, g, v)][:].rearrange("p (b m t) -> p m t b", b=2, t=PACK)
-                        nc.vector.tensor_copy(out=dst[:, :, v, 0:2, :], in_=half[:, :, 0:2, :])
-                        nc.scalar.copy(out=dst[:, :, v, 2:4, :], in_=half[:, :, 2:4, :])
+                        part = w1_raw[(e, g, v)][:].rearrange("p (a b) (m t) -> p m a t b", a=2, t=PACK)
+                        m0 = v * (P // 2)
+                        mv = LAST_VECTOR_M
+                        nc.vector.tensor_copy(out=dst[:, m0:m0 + mv], in_=part[:, 0:mv])
+                        nc.scalar.copy(out=dst[:, m0 + mv:m0 + P // 2], in_=part[:, mv:P // 2])
                     src = None
                 else:
                     src = w1_raw[(e, g)][:].rearrange("p (a b m t) -> p m a t b", a=2, b=2, t=PACK)
@@ -158,8 +162,10 @@ def tile_routed_moe_kernel(tc, xT, w1, w2, gate, offs, out):
                     nc.vector.tensor_copy(out=dst[:, :, :, 0:2, :], in_=src[:, :, :, 0:2, :])
                     nc.scalar.copy(out=dst[:, :, :, 2:4, :], in_=src[:, :, :, 2:4, :])
                 else:
-                    nc.scalar.copy(out=dst[:, P - ms:P], in_=src[:, P - ms:P])
-                    nc.vector.tensor_copy(out=dst[:, 0:P - ms], in_=src[:, 0:P - ms])
+                    if ms > 0:
+                        nc.scalar.copy(out=dst[:, P - ms:P], in_=src[:, P - ms:P])
+                    if ms < P:
+                        nc.vector.tensor_copy(out=dst[:, 0:P - ms], in_=src[:, 0:P - ms])
                 wc = keep.tile([P, H], U32, name="w1c%d%d" % (e, g), align_bytes=64)
                 ws = keep.tile([P, H], U8, name="w1s%d%d" % (e, g), align_bytes=64)
                 if last:
@@ -190,31 +196,33 @@ def tile_routed_moe_kernel(tc, xT, w1, w2, gate, offs, out):
             hg = keep.tile([P, C, PACK], BF16, name="hg%d" % e, align_bytes=64)
             hc = keep.tile([P, C], U32, name="hc%d" % e, align_bytes=64)
             hs = keep.tile([P, C], U8, name="hs%d" % e, align_bytes=64)
-            y = [psum_y.tile([P, C], F32, name="y%d%d" % (e, b), tag="y") for b in range(NB)]
+            parts = [(0, HALF), (HALF, C)] if e == E - 1 else [(0, C)]
             for half in range(2):
                 hslots = slice(half * HALF, (half + 1) * HALF)
                 nc.scalar.activation(out=hg[:, hslots, :], in_=acc[half][:].rearrange("p t s -> p s t"), func=GELU)
                 nc.vector.quantize_mx(
                     out=hc[:, hslots].bitcast(FP8X4), scales=hs[:, hslots],
                     in_=hg[:, hslots, :].rearrange("p s t -> p (s t)"))
+            for s0, s1 in parts:
                 for b in range(NB):
                     cols = slice(b * P, (b + 1) * P)
+                    y = psum_y.tile([P, s1 - s0], F32, name="y%d%d%d" % (e, b, s0), tag="y")
                     nc.tensor.matmul_mx(
-                        out=y[b][:, hslots],
+                        out=y[:],
                         lhsT=w2c[:, cols].bitcast(FP8X4), lhsT_scale=w2s[:, cols],
-                        rhs=hc[:, hslots].bitcast(FP8X4), rhs_scale=hs[:, hslots],
+                        rhs=hc[:, s0:s1].bitcast(FP8X4), rhs_scale=hs[:, s0:s1],
                         start=True, stop=True,
                     )
-            for b in range(NB):
-                y_sb = keep.tile([P, C], F32, name="ysb%d%d" % (e, b))
-                nc.scalar.copy(out=y_sb[:], in_=y[b][:])
-                y_tiles[(e, b)] = y_sb
+                    y_sb = keep.tile([P, s1 - s0], F32, name="ysb%d%d%d" % (e, b, s0))
+                    nc.scalar.copy(out=y_sb[:], in_=y[:])
+                    y_parts[(e, b)].append((s0, s1, y_sb))
 
         for e in range(E):
             for b in range(NB):
-                nc.vector.tensor_tensor(
-                    out=win[b][:].indirect(offs_t[:, e * (C // 16):(e + 1) * (C // 16)]),
-                    in0=y_tiles[(e, b)][:], in1=gate_t[e][:, b, :], op=MULT,
-                )
+                for s0, s1, y_sb in y_parts[(e, b)]:
+                    nc.vector.tensor_tensor(
+                        out=win[b][:].indirect(offs_t[:, (e * C + s0) // 16:(e * C + s1) // 16]),
+                        in0=y_sb[:], in1=gate_t[e][:, b, s0:s1], op=MULT,
+                    )
                 if e == E - 1:
                     nc.sync.dma_start(out=out[b * P:(b + 1) * P, :], in_=win[b][:])

from contextlib import ExitStack

import concourse.mybir as mybir

K, T, E, C, H, N = 2048, 1024, 2, 256, 512, 256
SLOTS = E * C
FLOPS = 2 * SLOTS * (K * H + H * N)

F32 = mybir.dt.float32
BF16 = mybir.dt.bfloat16
U32 = mybir.dt.uint32
U16 = mybir.dt.uint16
U8 = mybir.dt.uint8
I32 = mybir.dt.int32
FP8X4 = mybir.dt.float8_e4m3fn_x4
GELU = mybir.ActivationFunctionType.Gelu_apprx_tanh
MULT = mybir.AluOpType.mult
ADD = mybir.AluOpType.add

P = 128
PACK = 4
K_PASS = P * PACK
PASSES = K // K_PASS
NB = N // P

X_SCALAR_TOKENS = 768
RAW_BUFS = 10
SCALAR_M = [[96, 96, 96, 0], [0, 128, 128, 0]]
LAST_VECTOR_M = 40
HALF = C // 2


def tile_routed_moe_kernel(tc, xT, w1, w2, gate, offs, out):
    nc = tc.nc
    with ExitStack() as ctx:
        lists = ctx.enter_context(tc.tile_pool(name="lists", bufs=1))
        keep = ctx.enter_context(tc.tile_pool(name="keep", bufs=1))
        raw_pool = ctx.enter_context(tc.tile_pool(name="raw", bufs=RAW_BUFS))
        stage = ctx.enter_context(tc.tile_pool(name="stage", bufs=3))
        psum_a = ctx.enter_context(tc.psum_pool(name="psum_a", bufs=4))
        psum_y = ctx.enter_context(tc.psum_pool(name="psum_y", bufs=4))

        offs_t = lists.tile([P, SLOTS // 16], U16, name="offs_t")

        x_view = xT.rearrange("(g p u e) n -> g u p (e n)", p=P, u=2, e=2)
        w1_view = w1.rearrange("x (g p j) c -> x g p (j c)", p=P, j=PACK)
        x_raw = {}
        w1_raw = {}
        w2_raw = {}
        gate_t = {}

        def load_x(g, u):
            t = raw_pool.tile([P, 2 * T], F32, name="xraw%d%d" % (g, u), tag="raw")
            nc.sync.dma_start(out=t[:], in_=x_view[g, u])
            x_raw[(g, u)] = t

        def load_w1(e, g):
            if (e, g) == (E - 1, PASSES - 1):
                for v in range(2):
                    t = raw_pool.tile([P, PACK, H // 2], F32, name="w1raw%d%d%d" % (e, g, v), tag="raw")
                    nc.sync.dma_start(out=t[:], in_=w1[e, g * K_PASS:(g + 1) * K_PASS, v * (H // 2):(v + 1) * (H // 2)].rearrange("(p j) c -> p j c", j=PACK))
                    w1_raw[(e, g, v)] = t
                return
            t = raw_pool.tile([P, PACK * H], F32, name="w1raw%d%d" % (e, g), tag="raw")
            nc.sync.dma_start(out=t[:], in_=w1_view[e, g])
            w1_raw[(e, g)] = t

        def load_w2_gate(e):
            t = keep.tile([P, PACK, N], F32, name="w2raw%d" % e)
            nc.sync.dma_start(out=t[:], in_=w2[e].rearrange("(p j) n -> p j n", j=PACK))
            w2_raw[e] = t
            gt = keep.tile([P, NB, C], F32, name="gate%d" % e)
            nc.sync.dma_start(out=gt[:], in_=gate[:, e * C:(e + 1) * C].rearrange("(b p) s -> p b s", p=P))
            gate_t[e] = gt

        load_x(0, 0)
        nc.sync.dma_start(offs_t[:], offs)
        for g in range(PASSES):
            for u in range(2):
                if (g, u) != (0, 0):
                    load_x(g, u)
        for g in range(PASSES):
            load_w1(0, g)
        load_w2_gate(0)
        for g in range(PASSES):
            load_w1(1, g)
        load_w2_gate(1)

        warm_in = keep.tile([P, 8], F32, name="warm_in")
        warm_out = keep.tile([P, 8], F32, name="warm_out")
        nc.gpsimd.memset(warm_in[:], 0.0)
        nc.scalar.activation(out=warm_out[:], in_=warm_in[:], func=GELU)
        win = []
        for b in range(NB):
            wt = keep.tile([P, T], F32, name="win%d" % b)
            nc.gpsimd.memset(wt[:], 0.0)
            win.append(wt)

        x_codes = []
        x_scales = []
        x_words = {}
        x_grouped = {}

        def x_cast_gather(g, u):
            if u == 0:
                x_words[g] = stage.tile([P, 2, SLOTS, 2], BF16, name="xw", tag="xw", bufs=2)
            pairs = stage.tile([P, T, 2], BF16, name="pairs", tag="pairs", bufs=4)
            src = x_raw[(g, u)][:].rearrange("p (e n) -> p n e", e=2)
            cs = X_SCALAR_TOKENS
            nc.scalar.copy(out=pairs[:, 0:cs, :], in_=src[:, 0:cs, :])
            nc.gpsimd.tensor_scalar(out=pairs[:, cs:T, :], in0=src[:, cs:T, :], scalar1=1.0, scalar2=0.0, op0=MULT, op1=ADD)
            window = pairs[:].rearrange("p n e -> p (n e)").bitcast(U32)
            dst = x_words[g][:].rearrange("p u s e -> p (u s e)").bitcast(U32).rearrange("p (u s) -> p u s", u=2)
            nc.vector.tensor_copy(out=dst[:, u, :], in_=window.indirect(offs_t[:]))

        def x_interleave(g):
            xg = stage.tile([P, SLOTS, PACK], BF16, name="xg", tag="xg", bufs=2, align_bytes=64)
            nc.vector.tensor_copy(
                out=xg[:].rearrange("p s t -> p (s t)").bitcast(I32).rearrange("p (s u) -> p s u", u=2),
                in_=x_words[g][:].rearrange("p u s e -> p (u s e)").bitcast(I32).rearrange("p (u s) -> p s u", u=2),
            )
            x_grouped[g] = xg

        def x_quantize(g):
            xc = keep.tile([P, SLOTS], U32, name="xc%d" % g, align_bytes=64)
            xs = keep.tile([P, SLOTS], U8, name="xs%d" % g, align_bytes=64)
            nc.vector.quantize_mx(out=xc[:].bitcast(FP8X4), scales=xs[:], in_=x_grouped[g][:].rearrange("p s t -> p (s t)"))
            x_codes.append(xc)
            x_scales.append(xs)

        for g in range(PASSES):
            x_cast_gather(g, 0)
            if g > 0:
                x_interleave(g - 1)
            x_cast_gather(g, 1)
            if g > 0:
                x_quantize(g - 1)
        x_interleave(PASSES - 1)
        x_quantize(PASSES - 1)

        y_parts = {(e, b): [] for e in range(E) for b in range(NB)}
        for e in range(E):
            acc = [psum_a.tile([P, PACK, HALF], F32, name="a%d%d" % (e, half), tag="a") for half in range(2)]
            for g in range(PASSES):
                wg = stage.tile([P, PACK * H], BF16, name="wg", tag="wg", bufs=3, align_bytes=64)
                dst = wg[:].rearrange("p (t m a b) -> p m a t b", t=PACK, a=2, b=2)
                last = g == PASSES - 1
                ms = SCALAR_M[e][g]
                if (e, g) == (E - 1, PASSES - 1):
                    for v in range(2):
                        part = w1_raw[(e, g, v)][:].rearrange("p (a b) (m t) -> p m a t b", a=2, t=PACK)
                        m0 = v * (P // 2)
                        mv = LAST_VECTOR_M
                        nc.vector.tensor_copy(out=dst[:, m0:m0 + mv], in_=part[:, 0:mv])
                        nc.scalar.copy(out=dst[:, m0 + mv:m0 + P // 2], in_=part[:, mv:P // 2])
                    src = None
                else:
                    src = w1_raw[(e, g)][:].rearrange("p (a b m t) -> p m a t b", a=2, b=2, t=PACK)
                if src is None:
                    pass
                elif last:
                    nc.vector.tensor_copy(out=dst[:, :, :, 0:2, :], in_=src[:, :, :, 0:2, :])
                    nc.scalar.copy(out=dst[:, :, :, 2:4, :], in_=src[:, :, :, 2:4, :])
                else:
                    if ms > 0:
                        nc.scalar.copy(out=dst[:, P - ms:P], in_=src[:, P - ms:P])
                    if ms < P:
                        nc.vector.tensor_copy(out=dst[:, 0:P - ms], in_=src[:, 0:P - ms])
                wc = keep.tile([P, H], U32, name="w1c%d%d" % (e, g), align_bytes=64)
                ws = keep.tile([P, H], U8, name="w1s%d%d" % (e, g), align_bytes=64)
                if last:
                    for hf in range(2):
                        nc.vector.quantize_mx(
                            out=wc[:, hf * 256:(hf + 1) * 256].bitcast(FP8X4), scales=ws[:, hf * 256:(hf + 1) * 256],
                            in_=wg[:, hf * 1024:(hf + 1) * 1024])
                else:
                    nc.vector.quantize_mx(out=wc[:].bitcast(FP8X4), scales=ws[:], in_=wg[:])
                for pair in range(2):
                    for half in range(2):
                        hs0 = e * C + half * HALF
                        for t in (2 * pair, 2 * pair + 1):
                            cols = slice(t * P, (t + 1) * P)
                            nc.tensor.matmul_mx(
                                out=acc[half][:, t, :],
                                lhsT=wc[:, cols].bitcast(FP8X4), lhsT_scale=ws[:, cols],
                                rhs=x_codes[g][:, hs0:hs0 + HALF].bitcast(FP8X4), rhs_scale=x_scales[g][:, hs0:hs0 + HALF],
                                start=(g == 0 and t == 0), stop=(g == PASSES - 1 and t == PACK - 1),
                            )

            w2g = keep.tile([P, N, PACK], BF16, name="w2g%d" % e, align_bytes=64)
            nc.vector.tensor_copy(out=w2g[:].rearrange("p (c i) j -> p c j i", i=4), in_=w2_raw[e][:].rearrange("p j (c i) -> p c j i", i=4))
            w2c = keep.tile([P, N], U32, name="w2c%d" % e, align_bytes=64)
            w2s = keep.tile([P, N], U8, name="w2s%d" % e, align_bytes=64)
            nc.vector.quantize_mx(out=w2c[:].bitcast(FP8X4), scales=w2s[:], in_=w2g[:].rearrange("p n j -> p (n j)"))

            hg = keep.tile([P, C, PACK], BF16, name="hg%d" % e, align_bytes=64)
            hc = keep.tile([P, C], U32, name="hc%d" % e, align_bytes=64)
            hs = keep.tile([P, C], U8, name="hs%d" % e, align_bytes=64)
            parts = [(0, HALF), (HALF, C)] if e == E - 1 else [(0, C)]
            for half in range(2):
                hslots = slice(half * HALF, (half + 1) * HALF)
                nc.scalar.activation(out=hg[:, hslots, :], in_=acc[half][:].rearrange("p t s -> p s t"), func=GELU)
                nc.vector.quantize_mx(
                    out=hc[:, hslots].bitcast(FP8X4), scales=hs[:, hslots],
                    in_=hg[:, hslots, :].rearrange("p s t -> p (s t)"))
            for s0, s1 in parts:
                for b in range(NB):
                    cols = slice(b * P, (b + 1) * P)
                    y = psum_y.tile([P, s1 - s0], F32, name="y%d%d%d" % (e, b, s0), tag="y")
                    nc.tensor.matmul_mx(
                        out=y[:],
                        lhsT=w2c[:, cols].bitcast(FP8X4), lhsT_scale=w2s[:, cols],
                        rhs=hc[:, s0:s1].bitcast(FP8X4), rhs_scale=hs[:, s0:s1],
                        start=True, stop=True,
                    )
                    y_sb = keep.tile([P, s1 - s0], F32, name="ysb%d%d%d" % (e, b, s0))
                    nc.scalar.copy(out=y_sb[:], in_=y[:])
                    y_parts[(e, b)].append((s0, s1, y_sb))

        for e in range(E):
            for b in range(NB):
                for s0, s1, y_sb in y_parts[(e, b)]:
                    nc.vector.tensor_tensor(
                        out=win[b][:].indirect(offs_t[:, (e * C + s0) // 16:(e * C + s1) // 16]),
                        in0=y_sb[:], in1=gate_t[e][:, b, s0:s1], op=MULT,
                    )
                if e == E - 1:
                    nc.sync.dma_start(out=out[b * P:(b + 1) * P, :], in_=win[b][:])
